import numpy as np
import ml_dtypes


def mxq(x, axis, fmt="e4m3"):
    dtype, down = {"e4m3": (ml_dtypes.float8_e4m3fn, 7), "e5m2": (ml_dtypes.float8_e5m2, 14)}[fmt]
    v = np.moveaxis(np.asarray(x, np.float32).astype(ml_dtypes.bfloat16).astype(np.float64), axis, -1)
    blocks = v.reshape(v.shape[:-1] + (-1, 32))
    amax = np.abs(blocks).max(-1, keepdims=True)
    byte = np.maximum(np.where(amax > 0, np.frexp(amax)[1] - 1 + 127, 0) - down, 1)
    scale = np.exp2(byte - 127.0)
    codes = (blocks / scale).astype(np.float32).astype(dtype).astype(np.float64)
    return np.moveaxis((codes * scale).reshape(v.shape), -1, axis)


WIDE = False


def mx_kscale(k):
    if not WIDE:
        return np.ones(k)
    levels = np.array([30, -30])
    if k % 512:
        return np.exp2(np.random.permutation(np.resize(levels, k // 32))).repeat(32)
    a = np.empty((k // 512, 16))
    for p in range(k // 512):
        a[p, :8] = np.random.permutation(np.resize(levels, 8))
        for g in range(8):
            far = levels[np.abs(levels - a[p, g]) >= 10]
            a[p, g + 8] = far[np.random.randint(len(far))]
    return np.exp2(a.ravel()).repeat(32)


def f64(x):
    return np.asarray(x).astype(np.float64)


def striped(idx):
    return np.tile(np.asarray(idx).reshape(-1, 16).T, (8, 1)).astype(np.uint16)


def unstriped(offs):
    return offs[:16].T.reshape(-1).astype(np.int64)


E2M1 = np.array([0.0, 0.5, 1.0, 1.5, 2.0, 3.0, 4.0, 6.0, -0.0, -0.5, -1.0, -1.5, -2.0, -3.0, -4.0, -6.0])


def pack_weight(w, fmt):
    k, n = w.shape
    w = f64(np.asarray(w, np.float32).astype(ml_dtypes.bfloat16)).reshape(k // 32, 32, n)
    amax = np.abs(w).max(1)
    if fmt in ("e4m3", "e5m2"):
        byte = np.frexp(amax)[1] - 1 + 127 - (7 if fmt == "e4m3" else 14)
    else:
        mant, ex = np.frexp(amax / 6.0)
        byte = np.where(mant > 0.5, ex, ex - 1) + 127
    byte = np.clip(np.where(amax > 0, byte, 1), 1, 254)
    scaled = (w * np.exp2(127.0 - byte)[:, None, :]).reshape(k, n).astype(np.float32)
    by_word = np.ascontiguousarray(scaled.reshape(k // 512, 128, 4, n).transpose(0, 1, 3, 2))
    if fmt in ("e4m3", "e5m2"):
        words = by_word.astype(ml_dtypes.float8_e4m3fn if fmt == "e4m3" else ml_dtypes.float8_e5m2).view(np.uint8)
    else:
        c = by_word.astype(ml_dtypes.float4_e2m1fn).view(np.uint8) & 0xF
        words = (c[..., 0::2] | (c[..., 1::2] << 4)).reshape(k // 512, 128, 2 * n)
    return np.ascontiguousarray(words), np.ascontiguousarray(byte.astype(np.uint8).reshape(k // 512, 16, n))


def unpack_weight(words, scales, fmt):
    g, _, n = scales.shape
    words = np.ascontiguousarray(words).reshape(g, 128, n, -1)
    if fmt in ("e4m3", "e5m2"):
        vals = words.view(ml_dtypes.float8_e4m3fn if fmt == "e4m3" else ml_dtypes.float8_e5m2).astype(np.float64)
    else:
        nib = np.empty((g, 128, n, 4), np.uint8)
        nib[..., 0::2] = words & 0xF
        nib[..., 1::2] = words >> 4
        vals = E2M1[nib]
    vals = vals * np.repeat(np.exp2(scales.astype(np.float64) - 127.0), 8, axis=1)[..., None]
    return vals.transpose(0, 1, 3, 2).reshape(g * 512, n)


K, F, T, Z, J, R, N, S, E = 512, 512, 1024, 1024, 256, 512, 256, 1024, 1024


def setup_inputs():
    n = np.random.standard_normal
    idx = np.random.permutation(T)[:J]
    idx2 = np.random.permutation(Z)[:J]
    idx3 = np.random.permutation(J)[:J]
    idx4 = np.random.permutation(S)[:N]
    idx5 = np.random.permutation(E)[:J]
    fk = mx_kscale(K)
    fr = mx_kscale(R)
    ff = mx_kscale(F)
    xtp = pack_weight(n((K, T)) / fk[:, None], "e4m3")
    wp = pack_weight(n((K, R)) * 1 / np.sqrt(K) * fk[:, None] * fr, "e2m1")
    xop = pack_weight(n((F, Z)) / ff[:, None], "e2m1")
    w0p = pack_weight(n((F, R)) * 1 / np.sqrt(F) * ff[:, None] * fr, "e5m2")
    vsp = pack_weight(n((R, S)) * 1 / np.sqrt(R) / fr[:, None], "e5m2")
    return {
        "xt_words": xtp[0],
        "xt_scales": xtp[1],
        "w_words": wp[0],
        "w_scales": wp[1],
        "xo_words": xop[0],
        "xo_scales": xop[1],
        "w0_words": w0p[0],
        "w0_scales": w0p[1],
        "sa": (np.random.uniform(0.5, 1.6, (R, 1))).astype(np.float32),
        "vs_words": vsp[0],
        "vs_scales": vsp[1],
        "offs": striped(idx),
        "offs2": striped(idx2),
        "offs3": striped(idx3),
        "offs4": striped(idx4),
        "offs5": striped(idx5),
    }


def reference(xt_words, xt_scales, w_words, w_scales, xo_words, xo_scales, w0_words, w0_scales, sa, vs_words, vs_scales, offs, offs2, offs3, offs4, offs5):
    idx = unstriped(offs)
    idx2 = unstriped(offs2)
    idx3 = unstriped(offs3)
    idx4 = unstriped(offs4)
    idx5 = unstriped(offs5)
    xtu = unpack_weight(xt_words, xt_scales, "e4m3")
    wu = unpack_weight(w_words, w_scales, "e2m1")
    xou = unpack_weight(xo_words, xo_scales, "e2m1")
    w0u = unpack_weight(w0_words, w0_scales, "e5m2")
    vsu = unpack_weight(vs_words, vs_scales, "e5m2")
    xtidxg = xtu[:, idx]
    xoidx2g = xou[:, idx2]
    a = wu.T @ xtidxg + w0u.T @ xoidx2g
    hid = np.abs(a - a[:, idx3] * f64(sa))
    vsidx4g = vsu[:, idx4]
    hidq = mxq(hid, 0, "e4m3")
    p = vsidx4g.T @ hidq
    y = np.zeros((N, E))
    y[:, idx5] = p
    return y

@@ -1,0 +1,180 @@
+from contextlib import ExitStack
+
+import concourse.mybir as mybir
+
+FLOPS = 335544320
+
+F32 = mybir.dt.float32
+BF16 = mybir.dt.bfloat16
+I32 = mybir.dt.int32
+U32 = mybir.dt.uint32
+U16 = mybir.dt.uint16
+U8 = mybir.dt.uint8
+E4M3 = mybir.dt.float8_e4m3fn_x4
+E5M2 = mybir.dt.float8_e5m2_x4
+E2M1 = mybir.dt.float4_e2m1fn_x4
+ALU = mybir.AluOpType
+ACT = mybir.ActivationFunctionType
+
+P = 128
+PACK = 4
+QUADS = 4
+TABLE = 1024
+J = 256
+R = 512
+N = 256
+E = 1024
+HALF = J // 2
+
+
+def tile_list_lessneighbour_bank_store_scattered_kernel(
+    tc, xt_words, xt_scales, w_words, w_scales, xo_words, xo_scales, w0_words, w0_scales,
+    sa, vs_words, vs_scales, offs, offs2, offs3, offs4, offs5, out,
+):
+    nc = tc.nc
+    with ExitStack() as ctx:
+        sb = ctx.enter_context(tc.tile_pool(name="sb", bufs=1))
+        shared = ctx.enter_context(tc.tile_pool(name="shared", bufs=1))
+        ps = ctx.enter_context(tc.psum_pool(name="ps", bufs=1))
+
+        def tile(name, shape, dtype, tag=None):
+            return sb.tile(shape, dtype, name=name, tag=tag or name, align_bytes=64)
+
+        lists = [tile("list%d" % i, [P, J // 16], U16) for i in range(5)]
+        l_xt, l_xo, l_a, l_vs, l_out = lists
+        xt_w = tile("xt_w", [P, TABLE], U32)
+        xo_w = tile("xo_w", [P, TABLE], U16)
+        vs_w = tile("vs_w", [P, TABLE], U32)
+        xt_s = tile("xt_s", [P, TABLE], U8)
+        xo_s = tile("xo_s", [P, TABLE], U8)
+        vs_s = tile("vs_s", [P, TABLE], U8)
+        w_raw = tile("w_raw", [P, R], U16)
+        w0_raw = tile("w0_raw", [P, R], U32)
+        ws_stage = tile("ws_stage", [PACK, QUADS, 2 * R // 4], I32)
+        ws_rows = shared.tile([P, 2 * R], U8, name="ws_rows", align_bytes=64, offset=0)
+        ws = tile("ws", [P, 2 * R], U8)
+        w_p = tile("w_p", [P, R], U16)
+        w0_p = tile("w0_p", [P, R], U32)
+        sa_t = tile("sa_t", [P, PACK], F32)
+        pages = [tile("page%d" % i, [P, E], F32) for i in range(2)]
+
+        def words(ap):
+            return ap[0].rearrange("p c r -> p (c r)").bitcast(I32)
+
+        def load_rows(engine, plane, scales):
+            for q in range(QUADS):
+                engine.dma_start(plane[32 * q : 32 * q + 4, :].bitcast(I32), scales[0, 4 * q : 4 * q + 4, :].bitcast(I32))
+
+        for plane in (xt_s, xo_s, ws_rows, vs_s):
+            nc.vector.memset(plane[:].bitcast(I32), 0)
+
+        nc.gpsimd.dma_start(w_raw[:].bitcast(I32), w_words[0].bitcast(I32))
+        nc.gpsimd.dma_start(sa_t[:], sa.rearrange("(p t) o -> p (t o)", t=PACK))
+        nc.sync.dma_start(l_xt[:], offs)
+        for i, scales in enumerate((w_scales, w0_scales)):
+            nc.sync.dma_start(
+                ws_stage[:, :, i * (R // 4) : (i + 1) * (R // 4)],
+                scales[0].bitcast(I32).rearrange("(q r) c -> r q c", r=4),
+            )
+        load_rows(nc.scalar, xt_s, xt_scales)
+        nc.sync.dma_start(xt_w[:].bitcast(I32), words(xt_words))
+        nc.sync.dma_start(l_xo[:], offs2)
+        nc.sync.dma_start(w0_raw[:].bitcast(I32), words(w0_words))
+        nc.sync.dma_start(xo_w[:].bitcast(I32), xo_words[0].bitcast(I32))
+        load_rows(nc.scalar, xo_s, xo_scales)
+        nc.sync.dma_start(l_a[:], offs3)
+        nc.sync.dma_start(vs_w[:].bitcast(I32), words(vs_words))
+        nc.sync.dma_start(l_vs[:], offs4)
+        nc.sync.dma_start(l_out[:], offs5)
+        load_rows(nc.sync, vs_s, vs_scales)
+
+        for page in pages:
+            nc.vector.memset(page[:].bitcast(I32), 0)
+
+        for q in range(QUADS):
+            nc.vector.tensor_copy(ws_rows[32 * q : 32 * q + 4, :].bitcast(I32), ws_stage[:, q, :])
+        nc.vector.tensor_copy(
+            ws[:].rearrange("p (i t m) -> p i t m", i=2, t=PACK),
+            ws_rows[:].rearrange("p (i m t) -> p i t m", i=2, t=PACK),
+        )
+
+        def gather(got, window, offsets):
+            nc.vector.tensor_copy(got[:], window[:].indirect(offsets[:]))
+            return got
+
+        xt_gs = gather(tile("xt_gs", [P, J], U8), xt_s, l_xt)
+        xt_gw = gather(tile("xt_gw", [P, J], U32), xt_w, l_xt)
+        xo_gs = gather(shared.tile([P, J], U8, name="xo_gs", align_bytes=64, offset=0), xo_s, l_xo)
+        xo_gw = gather(shared.tile([P, J], U16, name="xo_gw", align_bytes=64, offset=J), xo_w, l_xo)
+
+        nc.scalar.copy(
+            w_p[:].rearrange("p (t m) -> p t m", t=PACK),
+            w_raw[:].rearrange("p (m t) -> p t m", t=PACK),
+        )
+        nc.scalar.copy(
+            w0_p[:].rearrange("p (t m) -> p m t", t=PACK),
+            w0_raw[:].rearrange("p (m t) -> p m t", t=PACK),
+        )
+
+        banks = [ps.tile([P, J], F32, name="a_ps%d" % t) for t in range(PACK)]
+        for t in range(PACK):
+            cols = slice(t * P, (t + 1) * P)
+            nc.tensor.matmul_mx(
+                banks[t][:], lhsT=w_p[:, cols].bitcast(E2M1), lhsT_scale=ws[:, cols],
+                rhs=xt_gw[:].bitcast(E4M3), rhs_scale=xt_gs[:], start=True, stop=False,
+            )
+        for t in range(PACK):
+            cols = slice(t * P, (t + 1) * P)
+            nc.tensor.matmul_mx(
+                banks[t][:], lhsT=w0_p[:, cols].bitcast(E5M2), lhsT_scale=ws[:, R + t * P : R + (t + 1) * P],
+                rhs=xo_gw[:].bitcast(E2M1), rhs_scale=xo_gs[:], start=False, stop=True,
+            )
+
+        rows = [tile("a%d" % t, [P, J], F32) for t in range(PACK)]
+        part = [tile("g%d" % t, [P, J], F32) for t in range(PACK)]
+        for t in range(PACK):
+            nc.vector.tensor_copy(rows[t][:], banks[t][:])
+            for h in range(2):
+                nc.scalar.activation(
+                    out=part[t][:, h * HALF : (h + 1) * HALF],
+                    in_=rows[t][:].indirect(l_a[:, h * (HALF // 16) : (h + 1) * (HALF // 16)]),
+                    func=ACT.Copy, scale=sa_t[:, t : t + 1],
+                )
+
+        diff = tile("diff", [P, PACK, J], F32)
+        halves = [slice(h * HALF, (h + 1) * HALF) for h in range(2)]
+        for t in range(PACK - 1):
+            nc.vector.tensor_tensor(diff[:, t, :], banks[t][:], part[t][:], ALU.subtract)
+        last = PACK - 1
+        for cols in halves:
+            nc.vector.tensor_tensor(diff[:, last, cols], banks[last][:, cols], part[last][:, cols], ALU.subtract)
+        vs_gw = gather(tile("vs_gw", [P, J], U32), vs_w, l_vs)
+        vs_gs = gather(tile("vs_gs", [P, J], U8), vs_s, l_vs)
+
+        hid = [tile("hid%d" % h, [P, HALF, PACK], BF16) for h in range(2)]
+        hid_w = [tile("hid_w0", [P, HALF], U32, "vs_w"), tile("hid_w1", [P, HALF], U32)]
+        hid_s = [tile("hid_s0", [P, HALF], U8, "vs_s"), tile("hid_s1", [P, HALF], U8)]
+        for h in range(2):
+            nc.scalar.activation(out=hid[h][:], in_=diff[:, :, halves[h]].rearrange("p t j -> p j t"), func=ACT.Abs)
+            nc.vector.quantize_mx(
+                out=hid_w[h][:].bitcast(E4M3), scales=hid_s[h][:], in_=hid[h][:].rearrange("p j t -> p (j t)")
+            )
+
+        for h in range(2):
+            places = l_out[:, h * (HALF // 16) : (h + 1) * (HALF // 16)]
+            for i in range(2):
+                cols = slice(i * P, (i + 1) * P)
+                p_ps = ps.tile([P, HALF], F32, name="p_ps%d%d" % (h, i))
+                nc.tensor.matmul_mx(
+                    p_ps[:], lhsT=vs_gw[:, cols].bitcast(E5M2), lhsT_scale=vs_gs[:, cols],
+                    rhs=hid_w[h][:].bitcast(E4M3), rhs_scale=hid_s[h][:], start=True, stop=True,
+                )
+                p_sb = tile("p_sb%d%d" % (h, i), [P, HALF], F32)
+                if i == 0:
+                    nc.scalar.copy(p_sb[:], p_ps[:])
+                    nc.scalar.activation(out=pages[i][:].indirect(places), in_=p_sb[:], func=ACT.Copy)
+                else:
+                    nc.vector.tensor_copy(p_sb[:], p_ps[:])
+                    nc.vector.tensor_copy(pages[i][:].indirect(places), p_sb[:])
+        nc.scalar.dma_start(out[:P, :], pages[0][:])
+        nc.sync.dma_start(out[P:, :], pages[1][:])

@@ -25,6 +25,9 @@ R = 512
 N = 256
 E = 1024
 HALF = J // 2
+XO_S = 2048
+VS_S = XO_S - 512
+VS_GW = XO_S + 512
 
 
 def tile_list_lessneighbour_bank_store_scattered_kernel(
@@ -46,8 +49,8 @@ def tile_list_lessneighbour_bank_store_scattered_kernel(
         xo_w = tile("xo_w", [P, TABLE], U16)
         vs_w = tile("vs_w", [P, TABLE], U32)
         xt_s = tile("xt_s", [P, TABLE], U8)
-        xo_s = tile("xo_s", [P, TABLE], U8)
-        vs_s = tile("vs_s", [P, TABLE], U8)
+        xo_s = shared.tile([P, TABLE], U8, name="xo_s", align_bytes=64, offset=XO_S)
+        vs_stage = tile("vs_stage", [32, QUADS, TABLE // 4], I32)
         w_raw = tile("w_raw", [P, R], U16)
         w0_raw = tile("w0_raw", [P, R], U32)
         ws_stage = tile("ws_stage", [PACK, QUADS, 2 * R // 4], I32)
@@ -56,7 +59,6 @@ def tile_list_lessneighbour_bank_store_scattered_kernel(
         w_p = tile("w_p", [P, R], U16)
         w0_p = tile("w0_p", [P, R], U32)
         sa_t = tile("sa_t", [P, PACK], F32)
-        pages = [tile("page%d" % i, [P, E], F32) for i in range(2)]
 
         def words(ap):
             return ap[0].rearrange("p c r -> p (c r)").bitcast(I32)
@@ -65,11 +67,13 @@ def tile_list_lessneighbour_bank_store_scattered_kernel(
             for q in range(QUADS):
                 engine.dma_start(plane[32 * q : 32 * q + 4, :].bitcast(I32), scales[0, 4 * q : 4 * q + 4, :].bitcast(I32))
 
-        for plane in (xt_s, xo_s, ws_rows, vs_s):
+        for plane in (xt_s, xo_s, ws_rows):
             nc.vector.memset(plane[:].bitcast(I32), 0)
+        nc.vector.memset(vs_stage[:], 0)
 
         nc.gpsimd.dma_start(w_raw[:].bitcast(I32), w_words[0].bitcast(I32))
-        nc.gpsimd.dma_start(sa_t[:], sa.rearrange("(p t) o -> p (t o)", t=PACK))
+        nc.gpsimd.dma_start(w0_raw[:].bitcast(I32), words(w0_words))
+        nc.gpsimd.dma_start(vs_stage[:4], vs_scales[0].bitcast(I32).rearrange("(q r) c -> r q c", r=4))
         nc.sync.dma_start(l_xt[:], offs)
         for i, scales in enumerate((w_scales, w0_scales)):
             nc.sync.dma_start(
@@ -79,17 +83,13 @@ def tile_list_lessneighbour_bank_store_scattered_kernel(
         load_rows(nc.scalar, xt_s, xt_scales)
         nc.sync.dma_start(xt_w[:].bitcast(I32), words(xt_words))
         nc.sync.dma_start(l_xo[:], offs2)
-        nc.sync.dma_start(w0_raw[:].bitcast(I32), words(w0_words))
         nc.sync.dma_start(xo_w[:].bitcast(I32), xo_words[0].bitcast(I32))
-        load_rows(nc.scalar, xo_s, xo_scales)
-        nc.sync.dma_start(l_a[:], offs3)
-        nc.sync.dma_start(vs_w[:].bitcast(I32), words(vs_words))
         nc.sync.dma_start(l_vs[:], offs4)
+        load_rows(nc.scalar, xo_s, xo_scales)
+        nc.sync.dma_start(vs_w[:].bitcast(I32), words(vs_words))
+        nc.sync.dma_start(l_a[:], offs3)
+        nc.sync.dma_start(sa_t[:], sa.rearrange("(p t) o -> p (t o)", t=PACK))
         nc.sync.dma_start(l_out[:], offs5)
-        load_rows(nc.sync, vs_s, vs_scales)
-
-        for page in pages:
-            nc.vector.memset(page[:].bitcast(I32), 0)
 
         for q in range(QUADS):
             nc.vector.tensor_copy(ws_rows[32 * q : 32 * q + 4, :].bitcast(I32), ws_stage[:, q, :])
@@ -104,8 +104,8 @@ def tile_list_lessneighbour_bank_store_scattered_kernel(
 
         xt_gs = gather(tile("xt_gs", [P, J], U8), xt_s, l_xt)
         xt_gw = gather(tile("xt_gw", [P, J], U32), xt_w, l_xt)
-        xo_gs = gather(shared.tile([P, J], U8, name="xo_gs", align_bytes=64, offset=0), xo_s, l_xo)
         xo_gw = gather(shared.tile([P, J], U16, name="xo_gw", align_bytes=64, offset=J), xo_w, l_xo)
+        xo_gs = gather(shared.tile([P, J], U8, name="xo_gs", align_bytes=64, offset=0), xo_s, l_xo)
 
         nc.scalar.copy(
             w_p[:].rearrange("p (t m) -> p t m", t=PACK),
@@ -130,32 +130,41 @@ def tile_list_lessneighbour_bank_store_scattered_kernel(
                 rhs=xo_gw[:].bitcast(E2M1), rhs_scale=xo_gs[:], start=False, stop=True,
             )
 
-        rows = [tile("a%d" % t, [P, J], F32) for t in range(PACK)]
-        part = [tile("g%d" % t, [P, J], F32) for t in range(PACK)]
-        for t in range(PACK):
+        pages = [tile("page0", [P, E], F32, "w0_p"), tile("page1", [P, E], F32, "ws")]
+        for page in pages:
+            nc.gpsimd.memset(page[:], 0.0)
+
+        vs_s = shared.tile([P, TABLE], U8, name="vs_s", align_bytes=64, offset=VS_S)
+        for q in range(QUADS):
+            nc.vector.tensor_copy(vs_s[32 * q : 32 * q + 32, :].bitcast(I32), vs_stage[:, q, :])
+        vs_gw = gather(shared.tile([P, J], U32, name="vs_gw", align_bytes=64, offset=VS_GW), vs_w, l_vs)
+        rows = [tile("a%d" % t, [P, J], F32, "vs_w" if t == 1 else None) for t in range(PACK)]
+        nc.scalar.copy(rows[0][:], banks[0][:])
+        for t in range(1, PACK):
             nc.vector.tensor_copy(rows[t][:], banks[t][:])
-            for h in range(2):
+        halves = [slice(h * HALF, (h + 1) * HALF) for h in range(2)]
+        diff = [tile("diff%d" % h, [P, PACK, HALF], F32) for h in range(2)]
+        hid = [tile("hid%d" % h, [P, HALF, PACK], BF16) for h in range(2)]
+
+        def differences(h):
+            for t in range(PACK):
+                part = tile("part%d%d" % (h, t), [P, HALF], F32, "part%d" % t if t in (1, 2) else None)
                 nc.scalar.activation(
-                    out=part[t][:, h * HALF : (h + 1) * HALF],
+                    out=part[:],
                     in_=rows[t][:].indirect(l_a[:, h * (HALF // 16) : (h + 1) * (HALF // 16)]),
                     func=ACT.Copy, scale=sa_t[:, t : t + 1],
                 )
+                nc.vector.tensor_tensor(diff[h][:, t, :], banks[t][:, halves[h]], part[:], ALU.subtract)
 
-        diff = tile("diff", [P, PACK, J], F32)
-        halves = [slice(h * HALF, (h + 1) * HALF) for h in range(2)]
-        for t in range(PACK - 1):
-            nc.vector.tensor_tensor(diff[:, t, :], banks[t][:], part[t][:], ALU.subtract)
-        last = PACK - 1
-        for cols in halves:
-            nc.vector.tensor_tensor(diff[:, last, cols], banks[last][:, cols], part[last][:, cols], ALU.subtract)
-        vs_gw = gather(tile("vs_gw", [P, J], U32), vs_w, l_vs)
-        vs_gs = gather(tile("vs_gs", [P, J], U8), vs_s, l_vs)
-
-        hid = [tile("hid%d" % h, [P, HALF, PACK], BF16) for h in range(2)]
-        hid_w = [tile("hid_w0", [P, HALF], U32, "vs_w"), tile("hid_w1", [P, HALF], U32)]
-        hid_s = [tile("hid_s0", [P, HALF], U8, "vs_s"), tile("hid_s1", [P, HALF], U8)]
+        differences(0)
+        vs_gs = gather(tile("vs_gs", [P, J], U8, "part03"), vs_s, l_vs)
+        differences(1)
         for h in range(2):
-            nc.scalar.activation(out=hid[h][:], in_=diff[:, :, halves[h]].rearrange("p t j -> p j t"), func=ACT.Abs)
+            nc.scalar.activation(out=hid[h][:], in_=diff[h][:].rearrange("p t j -> p j t"), func=ACT.Abs)
+
+        hid_w = [tile("hid_w%d" % h, [P, HALF], U32) for h in range(2)]
+        hid_s = [tile("hid_s%d" % h, [P, HALF], U8) for h in range(2)]
+        for h in range(2):
             nc.vector.quantize_mx(
                 out=hid_w[h][:].bitcast(E4M3), scales=hid_s[h][:], in_=hid[h][:].rearrange("p j t -> p (j t)")
             )

@@ -25,9 +25,8 @@ R = 512
 N = 256
 E = 1024
 HALF = J // 2
-XO_S = 2048
-VS_S = XO_S - 512
-VS_GW = XO_S + 512
+VS_S = 1024
+DIFF1 = VS_S + 512
 
 
 def tile_list_lessneighbour_bank_store_scattered_kernel(
@@ -49,8 +48,9 @@ def tile_list_lessneighbour_bank_store_scattered_kernel(
         xo_w = tile("xo_w", [P, TABLE], U16)
         vs_w = tile("vs_w", [P, TABLE], U32)
         xt_s = tile("xt_s", [P, TABLE], U8)
-        xo_s = shared.tile([P, TABLE], U8, name="xo_s", align_bytes=64, offset=XO_S)
-        vs_stage = tile("vs_stage", [32, QUADS, TABLE // 4], I32)
+        xo_s = tile("xo_s", [P, TABLE], U8)
+        vs_s = shared.tile([P, TABLE], U8, name="vs_s", align_bytes=64, offset=VS_S)
+        page0 = tile("page0", [P, E], F32)
         w_raw = tile("w_raw", [P, R], U16)
         w0_raw = tile("w0_raw", [P, R], U32)
         ws_stage = tile("ws_stage", [PACK, QUADS, 2 * R // 4], I32)
@@ -67,13 +67,12 @@ def tile_list_lessneighbour_bank_store_scattered_kernel(
             for q in range(QUADS):
                 engine.dma_start(plane[32 * q : 32 * q + 4, :].bitcast(I32), scales[0, 4 * q : 4 * q + 4, :].bitcast(I32))
 
-        for plane in (xt_s, xo_s, ws_rows):
+        for plane in (xt_s, xo_s, ws_rows, vs_s):
             nc.vector.memset(plane[:].bitcast(I32), 0)
-        nc.vector.memset(vs_stage[:], 0)
+        nc.vector.memset(page0[:].bitcast(I32), 0)
 
         nc.gpsimd.dma_start(w_raw[:].bitcast(I32), w_words[0].bitcast(I32))
         nc.gpsimd.dma_start(w0_raw[:].bitcast(I32), words(w0_words))
-        nc.gpsimd.dma_start(vs_stage[:4], vs_scales[0].bitcast(I32).rearrange("(q r) c -> r q c", r=4))
         nc.sync.dma_start(l_xt[:], offs)
         for i, scales in enumerate((w_scales, w0_scales)):
             nc.sync.dma_start(
@@ -89,6 +88,7 @@ def tile_list_lessneighbour_bank_store_scattered_kernel(
         nc.sync.dma_start(vs_w[:].bitcast(I32), words(vs_words))
         nc.sync.dma_start(l_a[:], offs3)
         nc.sync.dma_start(sa_t[:], sa.rearrange("(p t) o -> p (t o)", t=PACK))
+        load_rows(nc.sync, vs_s, vs_scales)
         nc.sync.dma_start(l_out[:], offs5)
 
         for q in range(QUADS):
@@ -130,20 +130,19 @@ def tile_list_lessneighbour_bank_store_scattered_kernel(
                 rhs=xo_gw[:].bitcast(E2M1), rhs_scale=xo_gs[:], start=False, stop=True,
             )
 
-        pages = [tile("page0", [P, E], F32, "w0_p"), tile("page1", [P, E], F32, "ws")]
-        for page in pages:
-            nc.gpsimd.memset(page[:], 0.0)
+        pages = [page0, tile("page1", [P, E], F32, "w0_p")]
+        nc.gpsimd.memset(pages[1][:], 0.0)
 
-        vs_s = shared.tile([P, TABLE], U8, name="vs_s", align_bytes=64, offset=VS_S)
-        for q in range(QUADS):
-            nc.vector.tensor_copy(vs_s[32 * q : 32 * q + 32, :].bitcast(I32), vs_stage[:, q, :])
-        vs_gw = gather(shared.tile([P, J], U32, name="vs_gw", align_bytes=64, offset=VS_GW), vs_w, l_vs)
+        vs_gw = gather(tile("vs_gw", [P, J], U32, "xo_s"), vs_w, l_vs)
         rows = [tile("a%d" % t, [P, J], F32, "vs_w" if t == 1 else None) for t in range(PACK)]
         nc.scalar.copy(rows[0][:], banks[0][:])
         for t in range(1, PACK):
             nc.vector.tensor_copy(rows[t][:], banks[t][:])
         halves = [slice(h * HALF, (h + 1) * HALF) for h in range(2)]
-        diff = [tile("diff%d" % h, [P, PACK, HALF], F32) for h in range(2)]
+        diff = [
+            tile("diff0", [P, PACK, HALF], F32),
+            shared.tile([P, PACK, HALF], F32, name="diff1", align_bytes=64, offset=DIFF1),
+        ]
         hid = [tile("hid%d" % h, [P, HALF, PACK], BF16) for h in range(2)]
 
         def differences(h):
@@ -163,7 +162,10 @@ def tile_list_lessneighbour_bank_store_scattered_kernel(
             nc.scalar.activation(out=hid[h][:], in_=diff[h][:].rearrange("p t j -> p j t"), func=ACT.Abs)
 
         hid_w = [tile("hid_w%d" % h, [P, HALF], U32) for h in range(2)]
-        hid_s = [tile("hid_s%d" % h, [P, HALF], U8) for h in range(2)]
+        hid_s = [
+            shared.tile([P, HALF], U8, name="hid_s0", align_bytes=64, offset=VS_S),
+            tile("hid_s1", [P, HALF], U8),
+        ]
         for h in range(2):
             nc.vector.quantize_mx(
                 out=hid_w[h][:].bitcast(E4M3), scales=hid_s[h][:], in_=hid[h][:].rearrange("p j t -> p (j t)")

from contextlib import ExitStack

import concourse.mybir as mybir

FLOPS = 335544320

F32 = mybir.dt.float32
BF16 = mybir.dt.bfloat16
I32 = mybir.dt.int32
U32 = mybir.dt.uint32
U16 = mybir.dt.uint16
U8 = mybir.dt.uint8
E4M3 = mybir.dt.float8_e4m3fn_x4
E5M2 = mybir.dt.float8_e5m2_x4
E2M1 = mybir.dt.float4_e2m1fn_x4
ALU = mybir.AluOpType
ACT = mybir.ActivationFunctionType

P = 128
PACK = 4
QUADS = 4
TABLE = 1024
J = 256
R = 512
N = 256
E = 1024
HALF = J // 2
VS_S = 1024
DIFF1 = VS_S + 512


def tile_list_lessneighbour_bank_store_scattered_kernel(
    tc, xt_words, xt_scales, w_words, w_scales, xo_words, xo_scales, w0_words, w0_scales,
    sa, vs_words, vs_scales, offs, offs2, offs3, offs4, offs5, out,
):
    nc = tc.nc
    with ExitStack() as ctx:
        sb = ctx.enter_context(tc.tile_pool(name="sb", bufs=1))
        shared = ctx.enter_context(tc.tile_pool(name="shared", bufs=1))
        ps = ctx.enter_context(tc.psum_pool(name="ps", bufs=1))

        def tile(name, shape, dtype, tag=None):
            return sb.tile(shape, dtype, name=name, tag=tag or name, align_bytes=64)

        lists = [tile("list%d" % i, [P, J // 16], U16) for i in range(5)]
        l_xt, l_xo, l_a, l_vs, l_out = lists
        xt_w = tile("xt_w", [P, TABLE], U32)
        xo_w = tile("xo_w", [P, TABLE], U16)
        vs_w = tile("vs_w", [P, TABLE], U32)
        xt_s = tile("xt_s", [P, TABLE], U8)
        xo_s = tile("xo_s", [P, TABLE], U8)
        vs_s = shared.tile([P, TABLE], U8, name="vs_s", align_bytes=64, offset=VS_S)
        page0 = tile("page0", [P, E], F32)
        w_raw = tile("w_raw", [P, R], U16)
        w0_raw = tile("w0_raw", [P, R], U32)
        ws_stage = tile("ws_stage", [PACK, QUADS, 2 * R // 4], I32)
        ws_rows = shared.tile([P, 2 * R], U8, name="ws_rows", align_bytes=64, offset=0)
        ws = tile("ws", [P, 2 * R], U8)
        w_p = tile("w_p", [P, R], U16)
        w0_p = tile("w0_p", [P, R], U32)
        sa_t = tile("sa_t", [P, PACK], F32)

        def words(ap):
            return ap[0].rearrange("p c r -> p (c r)").bitcast(I32)

        def load_rows(engine, plane, scales):
            for q in range(QUADS):
                engine.dma_start(plane[32 * q : 32 * q + 4, :].bitcast(I32), scales[0, 4 * q : 4 * q + 4, :].bitcast(I32))

        for plane in (xt_s, xo_s, ws_rows, vs_s):
            nc.vector.memset(plane[:].bitcast(I32), 0)
        nc.vector.memset(page0[:].bitcast(I32), 0)

        nc.gpsimd.dma_start(w_raw[:].bitcast(I32), w_words[0].bitcast(I32))
        nc.gpsimd.dma_start(w0_raw[:].bitcast(I32), words(w0_words))
        nc.sync.dma_start(l_xt[:], offs)
        for i, scales in enumerate((w_scales, w0_scales)):
            nc.sync.dma_start(
                ws_stage[:, :, i * (R // 4) : (i + 1) * (R // 4)],
                scales[0].bitcast(I32).rearrange("(q r) c -> r q c", r=4),
            )
        load_rows(nc.scalar, xt_s, xt_scales)
        nc.sync.dma_start(xt_w[:].bitcast(I32), words(xt_words))
        nc.sync.dma_start(l_xo[:], offs2)
        nc.sync.dma_start(xo_w[:].bitcast(I32), xo_words[0].bitcast(I32))
        nc.sync.dma_start(l_vs[:], offs4)
        load_rows(nc.scalar, xo_s, xo_scales)
        nc.sync.dma_start(vs_w[:].bitcast(I32), words(vs_words))
        nc.sync.dma_start(l_a[:], offs3)
        nc.sync.dma_start(sa_t[:], sa.rearrange("(p t) o -> p (t o)", t=PACK))
        load_rows(nc.sync, vs_s, vs_scales)
        nc.sync.dma_start(l_out[:], offs5)

        for q in range(QUADS):
            nc.vector.tensor_copy(ws_rows[32 * q : 32 * q + 4, :].bitcast(I32), ws_stage[:, q, :])
        nc.vector.tensor_copy(
            ws[:].rearrange("p (i t m) -> p i t m", i=2, t=PACK),
            ws_rows[:].rearrange("p (i m t) -> p i t m", i=2, t=PACK),
        )

        def gather(got, window, offsets):
            nc.vector.tensor_copy(got[:], window[:].indirect(offsets[:]))
            return got

        xt_gs = gather(tile("xt_gs", [P, J], U8), xt_s, l_xt)
        xt_gw = gather(tile("xt_gw", [P, J], U32), xt_w, l_xt)
        xo_gw = gather(shared.tile([P, J], U16, name="xo_gw", align_bytes=64, offset=J), xo_w, l_xo)
        xo_gs = gather(shared.tile([P, J], U8, name="xo_gs", align_bytes=64, offset=0), xo_s, l_xo)

        nc.scalar.copy(
            w_p[:].rearrange("p (t m) -> p t m", t=PACK),
            w_raw[:].rearrange("p (m t) -> p t m", t=PACK),
        )
        nc.scalar.copy(
            w0_p[:].rearrange("p (t m) -> p m t", t=PACK),
            w0_raw[:].rearrange("p (m t) -> p m t", t=PACK),
        )

        banks = [ps.tile([P, J], F32, name="a_ps%d" % t) for t in range(PACK)]
        for t in range(PACK):
            cols = slice(t * P, (t + 1) * P)
            nc.tensor.matmul_mx(
                banks[t][:], lhsT=w_p[:, cols].bitcast(E2M1), lhsT_scale=ws[:, cols],
                rhs=xt_gw[:].bitcast(E4M3), rhs_scale=xt_gs[:], start=True, stop=False,
            )
        for t in range(PACK):
            cols = slice(t * P, (t + 1) * P)
            nc.tensor.matmul_mx(
                banks[t][:], lhsT=w0_p[:, cols].bitcast(E5M2), lhsT_scale=ws[:, R + t * P : R + (t + 1) * P],
                rhs=xo_gw[:].bitcast(E2M1), rhs_scale=xo_gs[:], start=False, stop=True,
            )

        pages = [page0, tile("page1", [P, E], F32, "w0_p")]
        nc.gpsimd.memset(pages[1][:], 0.0)

        vs_gw = gather(tile("vs_gw", [P, J], U32, "xo_s"), vs_w, l_vs)
        rows = [tile("a%d" % t, [P, J], F32, "vs_w" if t == 1 else None) for t in range(PACK)]
        nc.scalar.copy(rows[0][:], banks[0][:])
        for t in range(1, PACK):
            nc.vector.tensor_copy(rows[t][:], banks[t][:])
        halves = [slice(h * HALF, (h + 1) * HALF) for h in range(2)]
        diff = [
            tile("diff0", [P, PACK, HALF], F32),
            shared.tile([P, PACK, HALF], F32, name="diff1", align_bytes=64, offset=DIFF1),
        ]
        hid = [tile("hid%d" % h, [P, HALF, PACK], BF16) for h in range(2)]

        def differences(h):
            for t in range(PACK):
                part = tile("part%d%d" % (h, t), [P, HALF], F32, "part%d" % t if t in (1, 2) else None)
                nc.scalar.activation(
                    out=part[:],
                    in_=rows[t][:].indirect(l_a[:, h * (HALF // 16) : (h + 1) * (HALF // 16)]),
                    func=ACT.Copy, scale=sa_t[:, t : t + 1],
                )
                nc.vector.tensor_tensor(diff[h][:, t, :], banks[t][:, halves[h]], part[:], ALU.subtract)

        differences(0)
        vs_gs = gather(tile("vs_gs", [P, J], U8, "part03"), vs_s, l_vs)
        differences(1)
        for h in range(2):
            nc.scalar.activation(out=hid[h][:], in_=diff[h][:].rearrange("p t j -> p j t"), func=ACT.Abs)

        hid_w = [tile("hid_w%d" % h, [P, HALF], U32) for h in range(2)]
        hid_s = [
            shared.tile([P, HALF], U8, name="hid_s0", align_bytes=64, offset=VS_S),
            tile("hid_s1", [P, HALF], U8),
        ]
        for h in range(2):
            nc.vector.quantize_mx(
                out=hid_w[h][:].bitcast(E4M3), scales=hid_s[h][:], in_=hid[h][:].rearrange("p j t -> p (j t)")
            )

        for h in range(2):
            places = l_out[:, h * (HALF // 16) : (h + 1) * (HALF // 16)]
            for i in range(2):
                cols = slice(i * P, (i + 1) * P)
                p_ps = ps.tile([P, HALF], F32, name="p_ps%d%d" % (h, i))
                nc.tensor.matmul_mx(
                    p_ps[:], lhsT=vs_gw[:, cols].bitcast(E5M2), lhsT_scale=vs_gs[:, cols],
                    rhs=hid_w[h][:].bitcast(E4M3), rhs_scale=hid_s[h][:], start=True, stop=True,
                )
                p_sb = tile("p_sb%d%d" % (h, i), [P, HALF], F32)
                if i == 0:
                    nc.scalar.copy(p_sb[:], p_ps[:])
                    nc.scalar.activation(out=pages[i][:].indirect(places), in_=p_sb[:], func=ACT.Copy)
                else:
                    nc.vector.tensor_copy(p_sb[:], p_ps[:])
                    nc.vector.tensor_copy(pages[i][:].indirect(places), p_sb[:])
        nc.scalar.dma_start(out[:P, :], pages[0][:])
        nc.sync.dma_start(out[P:, :], pages[1][:])
